import numpy as np
import ml_dtypes


def mxq(x, axis, fmt="e4m3"):
    dtype, down = {"e4m3": (ml_dtypes.float8_e4m3fn, 7), "e5m2": (ml_dtypes.float8_e5m2, 14)}[fmt]
    v = np.moveaxis(np.asarray(x, np.float32).astype(ml_dtypes.bfloat16).astype(np.float64), axis, -1)
    blocks = v.reshape(v.shape[:-1] + (-1, 32))
    amax = np.abs(blocks).max(-1, keepdims=True)
    byte = np.maximum(np.where(amax > 0, np.frexp(amax)[1] - 1 + 127, 0) - down, 1)
    scale = np.exp2(byte - 127.0)
    codes = (blocks / scale).astype(np.float32).astype(dtype).astype(np.float64)
    return np.moveaxis((codes * scale).reshape(v.shape), -1, axis)


WIDE = False


def mx_kscale(k):
    if not WIDE:
        return np.ones(k)
    levels = np.array([10, -10, 5, -5, 0])
    if k % 512:
        return np.exp2(np.random.permutation(np.resize(levels, k // 32))).repeat(32)
    a = np.empty((k // 512, 16))
    for p in range(k // 512):
        a[p, :8] = np.random.permutation(np.resize(levels, 8))
        for g in range(8):
            far = levels[np.abs(levels - a[p, g]) >= 10]
            a[p, g + 8] = far[np.random.randint(len(far))]
    return np.exp2(a.ravel()).repeat(32)


def f64(x):
    return np.asarray(x).astype(np.float64)


def striped(idx):
    return np.tile(idx.reshape(-1, 16).T, (8, 1)).astype(np.uint16)


def unstriped(offs):
    return offs[:16].T.reshape(-1).astype(np.int64)


E2M1 = np.array([0.0, 0.5, 1.0, 1.5, 2.0, 3.0, 4.0, 6.0, -0.0, -0.5, -1.0, -1.5, -2.0, -3.0, -4.0, -6.0])


def pack_weight(w, fmt):
    k, n = w.shape
    w = f64(np.asarray(w, np.float32).astype(ml_dtypes.bfloat16)).reshape(k // 32, 32, n)
    amax = np.abs(w).max(1)
    if fmt == "e4m3":
        byte = np.frexp(amax)[1] - 1 + 127 - 7
    else:
        mant, ex = np.frexp(amax / 6.0)
        byte = np.where(mant > 0.5, ex, ex - 1) + 127
    byte = np.clip(np.where(amax > 0, byte, 1), 1, 254)
    scaled = (w * np.exp2(127.0 - byte)[:, None, :]).reshape(k, n).astype(np.float32)
    by_word = np.ascontiguousarray(scaled.reshape(k // 512, 128, 4, n).transpose(0, 1, 3, 2))
    if fmt == "e4m3":
        words = by_word.astype(ml_dtypes.float8_e4m3fn).view(np.uint8)
    else:
        c = by_word.astype(ml_dtypes.float4_e2m1fn).view(np.uint8) & 0xF
        words = (c[..., 0::2] | (c[..., 1::2] << 4)).reshape(k // 512, 128, 2 * n)
    return np.ascontiguousarray(words), np.ascontiguousarray(byte.astype(np.uint8).reshape(k // 512, 16, n))


def unpack_weight(words, scales, fmt):
    g, _, n = scales.shape
    words = np.ascontiguousarray(words).reshape(g, 128, n, -1)
    if fmt == "e4m3":
        vals = words.view(ml_dtypes.float8_e4m3fn).astype(np.float64)
    else:
        nib = np.empty((g, 128, n, 4), np.uint8)
        nib[..., 0::2] = words & 0xF
        nib[..., 1::2] = words >> 4
        vals = E2M1[nib]
    vals = vals * np.repeat(np.exp2(scales.astype(np.float64) - 127.0), 8, axis=1)[..., None]
    return vals.transpose(0, 1, 3, 2).reshape(g * 512, n)


def gelu(v):
    return 0.5 * v * (1.0 + np.tanh(np.sqrt(2.0 / np.pi) * (v + 0.044715 * v**3)))


def bf(x):
    return np.asarray(x, np.float32).astype(ml_dtypes.bfloat16)


def planes(Y):
    n, m = Y.shape
    b = f64(bf(Y)).reshape(n // 32, 32, m)
    amax = np.abs(b).max(1)
    byte = np.clip(np.where(amax > 0, np.frexp(amax)[1] - 1 + 127 - 7, 1), 1, 254)
    codes = (b * np.exp2(127.0 - byte)[:, None, :]).reshape(n, m).astype(np.float32).astype(ml_dtypes.float8_e4m3fn).view(np.uint8)
    words = codes.reshape(n // 512, 128, 4, m).transpose(0, 1, 3, 2)
    return np.ascontiguousarray(words), np.ascontiguousarray(byte.astype(np.uint8).reshape(n // 512, 16, m))


K, T, S, T2, H, N = 1024, 2048, 512, 1024, 1536, 512

def setup_inputs():
    n = np.random.standard_normal
    s, u = mx_kscale(K)[:, None], mx_kscale(H)[:, None]
    tab_words, tab_scales = pack_weight(n((K, T)) * s, "e4m3")
    w2_words, w2_scales = pack_weight(0.7 * n((K, H)) / np.sqrt(K) / s, "e2m1")
    w3 = 0.7 * n((H, N)) / np.sqrt(H) * np.exp(0.8 * n(N)) / u
    w3_words, w3_scales = pack_weight(w3, "e4m3")
    return {
        "tab_words": tab_words, "tab_scales": tab_scales,
        "offs": striped(np.random.permutation(T)[:S]),
        "w1": (0.7 * n((K, H)) / np.sqrt(K) / s).astype(np.float32),
        "w2_words": w2_words, "w2_scales": w2_scales,
        "offs2": striped(np.random.permutation(T2)[:S]),
        "offs3": striped(np.random.permutation(T2)[:S]),
        "wg1": np.exp(0.3 * n((128, S))).astype(np.float32),
        "wg2": np.exp(0.3 * n((128, S))).astype(np.float32),
        "vol": (np.exp(0.5 * n((H, T2))) * u).astype(np.float32),
        "w3_words": w3_words, "w3_scales": w3_scales,
    }

def reference(tab_words, tab_scales, offs, w1, w2_words, w2_scales, offs2, offs3,
              wg1, wg2, vol, w3_words, w3_scales):
    v = unpack_weight(tab_words, tab_scales, "e4m3")[:, unstriped(offs)]
    h1 = mxq(f64(w1), 0, "e4m3").T @ v
    h2 = unpack_weight(w2_words, w2_scales, "e2m1").T @ v
    pageA = np.zeros((H, T2))
    pageA[:, unstriped(offs2)] = np.tile(f64(wg1), (H // 128, 1)) * h1
    pageB = np.zeros((H, T2))
    pageB[:, unstriped(offs3)] = np.tile(f64(wg2), (H // 128, 1)) * h2
    z = (1.0 + pageA) * (1.0 + pageB) * f64(vol)
    y = unpack_weight(w3_words, w3_scales, "e4m3").T @ mxq(z, 0, "e4m3")
    words, scales = planes(y)
    return y, words, scales

@@ -1,0 +1,323 @@
+from contextlib import ExitStack
+
+import concourse.mybir as mybir
+
+K, T, S, T2, H, N = 1024, 2048, 512, 1024, 1536, 512
+FLOPS = 2 * (2 * K * H * S + H * N * T2)
+
+F32 = mybir.dt.float32
+BF16 = mybir.dt.bfloat16
+I32 = mybir.dt.int32
+U32 = mybir.dt.uint32
+U16 = mybir.dt.uint16
+U8 = mybir.dt.uint8
+E4 = mybir.dt.float8_e4m3fn_x4
+E2 = mybir.dt.float4_e2m1fn_x4
+MULT = mybir.AluOpType.mult
+ADD = mybir.AluOpType.add
+COPY = mybir.ActivationFunctionType.Copy
+
+P = 128
+KA = K // 512
+HB = H // 512
+SLICES = H // P
+HALF = 512
+B_LEAD = 3
+
+
+def tile_list_luggage_slot_features_kernel(
+    tc, tab_words, tab_scales, offs, w1, w2_words, w2_scales, offs2, offs3,
+    wg1, wg2, vol, w3_words, w3_scales, out_0, out_1, out_2,
+):
+    nc = tc.nc
+    with ExitStack() as ctx:
+        lists = ctx.enter_context(tc.tile_pool(name="lists", bufs=1))
+        held = ctx.enter_context(tc.tile_pool(name="held", bufs=1))
+        ring = ctx.enter_context(tc.tile_pool(name="ring", bufs=2))
+        psum = ctx.enter_context(tc.psum_pool(name="psum", bufs=1))
+
+        idx = lists.tile([P, S // 16], U16, name="idx")
+        idx_a = lists.tile([P, S // 16], U16, name="idx_a")
+        idx_b = lists.tile([P, S // 16], U16, name="idx_b")
+
+        tab_s = held.tile([P, KA, T], U8, name="tab_s", align_bytes=64)
+        w2_s_raw = held.tile([P, KA, H], U8, name="w2_s_raw", align_bytes=64)
+        w3_s_raw = held.tile([P, N], U8, name="w3_s_raw", align_bytes=64)
+        nc.vector.memset(tab_s[:].bitcast(I32), 0)
+        nc.gpsimd.memset(w2_s_raw[:].bitcast(I32), 0)
+        nc.gpsimd.memset(w3_s_raw[:].bitcast(I32), 0)
+        pages = {}
+        for side in "BA":
+            pages[side] = [held.tile([P, T2], F32, name=f"page_{side}{i}") for i in range(2)]
+            for page in pages[side]:
+                nc.vector.memset(page[:], 0.0)
+
+        nc.sync.dma_start(idx[:], offs)
+        w2_raw = held.tile([P, KA, H // 2], I32, name="w2_raw", tag="raw_words", align_bytes=64)
+        nc.sync.dma_start(w2_raw[:], w2_words.rearrange("a p c -> p a c").bitcast(I32))
+        tab_w = [held.tile([P, T], I32, name=f"tab_w{a}", align_bytes=64) for a in range(KA)]
+
+        def load_tab_words(a):
+            nc.sync.dma_start(tab_w[a][:], tab_words[a].rearrange("p t i -> p (t i)").bitcast(I32))
+
+        load_tab_words(0)
+        for q in range(4):
+            nc.sync.dma_start(
+                tab_s[32 * q : 32 * q + 4, :, :].bitcast(I32),
+                tab_scales[:, 4 * q : 4 * q + 4, :].rearrange("a r c -> r a c").bitcast(I32),
+            )
+        load_tab_words(1)
+        for q in range(4):
+            nc.sync.dma_start(
+                w2_s_raw[32 * q : 32 * q + 4, :, :].bitcast(I32),
+                w2_scales[:, 4 * q : 4 * q + 4, :].rearrange("a r c -> r a c").bitcast(I32),
+            )
+        nc.sync.dma_start(idx_b[:], offs3)
+
+        gains = {}
+
+        def load_gains(side, wg):
+            gain = held.tile([P, 4, S], F32, name=f"gain_{side}")
+            for q in range(4):
+                nc.sync.dma_start(gain[32 * q : 32 * q + 32, :, :], wg.rearrange("(p t) j -> p t j", t=4))
+            gains[side] = gain
+
+        load_gains("B", wg2)
+
+        nc.sync.dma_start(idx_a[:], offs2)
+        w2_w, w2_s = {}, {}
+
+        def deal_w2(b):
+            cols = slice(512 * b, 512 * (b + 1))
+            words = held.tile([P, KA, 4, P], U16, name=f"w2_w{b}", align_bytes=64)
+            nc.vector.tensor_copy(
+                words[:].rearrange("p a t m -> p a m t"),
+                w2_raw[:].bitcast(U16)[:, :, cols].rearrange("p a (m t) -> p a m t", t=4),
+            )
+            scales = held.tile([P, KA, 4, P], U8, name=f"w2_s{b}", align_bytes=64)
+            nc.gpsimd.tensor_copy(
+                scales[:].rearrange("p a t m -> p a m t"),
+                w2_s_raw[:, :, cols].rearrange("p a (m t) -> p a m t", t=4),
+            )
+            w2_w[b], w2_s[b] = words, scales
+
+        deal_w2(0)
+        v_w, v_s = [], []
+        for a in range(KA):
+            words = held.tile([P, S], I32, name=f"v_w{a}", align_bytes=64)
+            scales = held.tile([P, S], U8, name=f"v_s{a}", align_bytes=64)
+            nc.vector.tensor_copy(scales[:], tab_s[:, a, :].indirect(idx[:]))
+            nc.vector.tensor_copy(words[:].bitcast(U32), tab_w[a][:].bitcast(U32).indirect(idx[:]))
+            v_w.append(words)
+            v_s.append(scales)
+
+        w1_w, w1_s = {}, {}
+
+        def prepare_w1(b):
+            for a in range(KA):
+                raw = ring.tile([P, 4, 512], F32, name="w1_raw", tag="wide_f32")
+                nc.sync.dma_start(
+                    raw[:],
+                    w1[512 * a : 512 * (a + 1), 512 * b : 512 * (b + 1)].rearrange("(p i) c -> p i c", i=4),
+                )
+                rounded = ring.tile([P, 4, P, 4], BF16, name="w1_bf", tag="wide_bf16", align_bytes=64)
+                nc.scalar.copy(
+                    rounded[:].rearrange("p t m i -> p m t i"),
+                    raw[:].rearrange("p i (m t) -> p m t i", t=4),
+                )
+                words = held.tile([P, 512], U32, name=f"w1_w{a}{b}", align_bytes=64)
+                scales = held.tile([P, 512], U8, name=f"w1_s{a}{b}", align_bytes=64)
+                nc.vector.quantize_mx(
+                    out=words[:].bitcast(E4), scales=scales[:], in_=rounded[:].rearrange("p t m i -> p (t m i)")
+                )
+                w1_w[a, b], w1_s[a, b] = words, scales
+
+        w3 = {}
+
+        def prepare_w3():
+            raw = held.tile([P, HB, N], I32, name="w3_raw", tag="raw_words", align_bytes=64)
+            nc.sync.dma_start(raw[:], w3_words.rearrange("a p c i -> p a (c i)").bitcast(I32))
+            for q in range(4):
+                nc.sync.dma_start(
+                    w3_s_raw[32 * q : 32 * q + 4 * HB, :].bitcast(I32),
+                    w3_scales[:, 4 * q : 4 * q + 4, :].bitcast(I32),
+                )
+            words = held.tile([P, HB, 4, P], I32, name="w3_w", align_bytes=64)
+            nc.vector.tensor_copy(
+                words[:].rearrange("p a t m -> p a m t"), raw[:].rearrange("p a (m t) -> p a m t", t=4)
+            )
+            scales = held.tile([P, 4, P], U8, name="w3_s", align_bytes=64)
+            nc.vector.tensor_copy(
+                scales[:].rearrange("p t m -> p m t"), w3_s_raw[:].rearrange("p (m t) -> p m t", t=4)
+            )
+            w3["w"], w3["s"] = words, scales
+
+        steps = [("B", s) for s in range(B_LEAD)]
+        for s in range(SLICES):
+            steps.append(("A", s))
+            if s + B_LEAD < SLICES:
+                steps.append(("B", s + B_LEAD))
+        last = len(steps) - 1
+
+        h_sb, gained, weighted, z4 = {}, {}, {}, {}
+        vols = {}
+
+        def load_vol(s):
+            b, t = divmod(s, 4)
+            rows = ring.tile([P, T2], F32, name="vol_rows", bufs=4)
+            nc.sync.dma_start(rows[:], vol[512 * b : 512 * (b + 1), :].rearrange("(p t) m -> p t m", t=4)[:, t, :])
+            vols[s] = rows
+
+        def first_product(k):
+            side, s = steps[k]
+            b, t = divmod(s, 4)
+            bank = psum.tile([P, S], F32, name="h_bank", tag=f"bank{k % 4}")
+            for a in range(KA):
+                if side == "B":
+                    lhs = w2_w[b][:, a, t, :].bitcast(E2)
+                    lhs_s = w2_s[b][:, a, t, :]
+                else:
+                    lhs = w1_w[a, b][:, P * t : P * (t + 1)].bitcast(E4)
+                    lhs_s = w1_s[a, b][:, P * t : P * (t + 1)]
+                nc.tensor.matmul_mx(
+                    out=bank[:], lhsT=lhs, lhsT_scale=lhs_s, rhs=v_w[a][:].bitcast(E4), rhs_scale=v_s[a][:],
+                    start=(a == 0), stop=(a == KA - 1),
+                )
+            h = ring.tile([P, S], F32, name="h_sb", bufs=3)
+            nc.scalar.copy(h[:], bank[:])
+            h_sb[k] = h
+
+        def gain_product(k):
+            side, s = steps[k]
+            if k == 0:
+                return
+            g = ring.tile([P, S], F32, name="gained", bufs=3)
+            nc.gpsimd.tensor_tensor(g[:], h_sb[k][:], gains[side][:, s % 4, :], MULT)
+            gained[k] = g
+
+        def page_of(k):
+            side, s = steps[k]
+            return pages[side][s % 2]
+
+        def scatter(k):
+            side, s = steps[k]
+            where = page_of(k)[:].indirect((idx_a if side == "A" else idx_b)[:])
+            if k == 0:
+                nc.vector.tensor_tensor(where, h_sb[k][:], gains[side][:, s % 4, :], MULT)
+            else:
+                nc.vector.tensor_copy(where, gained[k][:])
+
+        z_w, z_s = {}, {}
+        y_banks = {}
+
+        def last_pass(b, half):
+            for t in range(4):
+                if b == 0:
+                    y_banks[half, t] = psum.tile(
+                        [P, HALF], F32, name="y_bank", tag=f"bank{4 + t if half == 0 else t}"
+                    )
+                nc.tensor.matmul_mx(
+                    out=y_banks[half, t][:],
+                    lhsT=w3["w"][:, b, t, :].bitcast(E4), lhsT_scale=w3["s"][4 * b : P, t, :],
+                    rhs=z_w[b, half][:].bitcast(E4), rhs_scale=z_s[b, half][:],
+                    start=(b == 0), stop=(b == HB - 1),
+                )
+
+        def interleave(engine_copy, dst, src):
+            engine_copy(dst.rearrange("p (c i) t -> p c t i", i=4), src.rearrange("p t (c i) -> p c t i", i=4))
+
+        def quantise_z(b, half, engine_copy):
+            woven = ring.tile([P, HALF, 4], BF16, name="z_woven", align_bytes=64)
+            interleave(engine_copy, woven[:], z4[b][half][:])
+            words = held.tile([P, HALF], U32, name=f"z_w{b}{half}", align_bytes=64)
+            scales = held.tile([P, HALF], U8, name=f"z_s{b}{half}", align_bytes=64)
+            nc.vector.quantize_mx(
+                out=words[:].bitcast(E4), scales=scales[:], in_=woven[:].rearrange("p m t -> p (m t)")
+            )
+            z_w[b, half], z_s[b, half] = words, scales
+
+        def combine(k):
+            side, s = steps[k]
+            b, t = divmod(s, 4)
+            page = page_of(k)
+            if side == "B":
+                u = ring.tile([P, T2], F32, name="weighted", bufs=5)
+                nc.scalar.activation(u[:], page[:], COPY, bias=1.0)
+                nc.gpsimd.tensor_tensor(u[:], u[:], vols[s][:], MULT)
+                weighted[s] = u
+                return
+            if t == 0:
+                z4[b] = [ring.tile([P, 4, HALF], BF16, name="z_rows", bufs=4) for half in range(2)]
+            if k == last:
+                for half in range(2):
+                    cols = slice(HALF * half, HALF * (half + 1))
+                    nc.vector.scalar_tensor_tensor(
+                        z4[b][half][:, t, :], page[:, cols], 1.0, weighted[s][:, cols], ADD, MULT
+                    )
+            else:
+                one_plus = ring.tile([P, T2], F32, name="one_plus", bufs=2)
+                nc.scalar.activation(one_plus[:], page[:], COPY, bias=1.0)
+                for half in range(2):
+                    cols = slice(HALF * half, HALF * (half + 1))
+                    nc.gpsimd.tensor_tensor(z4[b][half][:, t, :], one_plus[:, cols], weighted[s][:, cols], MULT)
+            if t == 3 and k != last:
+                for half in range(2):
+                    quantise_z(b, half, nc.scalar.copy)
+                last_pass(b, 0)
+
+        deal_w2(1)
+        deal_w2(2)
+        prepare_w1(0)
+        load_gains("A", wg1)
+        for s in range(4):
+            load_vol(s)
+        prepare_w3()
+
+        for tick in range(-3, len(steps)):
+            k = tick + 3
+            if k <= last:
+                first_product(k)
+            k = tick + 2
+            if 0 <= k <= last:
+                gain_product(k)
+            k = tick + 1
+            if 0 <= k <= last:
+                scatter(k)
+            if tick >= 0:
+                side, s = steps[tick]
+                if tick == last:
+                    for b in range(HB - 1):
+                        last_pass(b, 1)
+                combine(tick)
+                if side == "B" and s + 4 < SLICES:
+                    load_vol(s + 4)
+                if side == "B" and s in (1, 5):
+                    prepare_w1(s // 4 + 1)
+
+        b = HB - 1
+        quantise_z(b, 0, nc.vector.tensor_copy)
+        quantise_z(b, 1, nc.scalar.copy)
+        y_w = held.tile([P, T2], U32, name="y_w", align_bytes=64)
+        y_s = held.tile([P, T2], U8, name="y_s", align_bytes=64)
+        y_rows = out_0.rearrange("(p t) m -> p t m", t=4)
+        for half in range(2):
+            last_pass(b, half)
+        for half in range(2):
+            cols = slice(HALF * half, HALF * (half + 1))
+            y = ring.tile([P, 4, HALF], F32, name="y", tag="wide_f32")
+            for t in range(4):
+                copy_out = nc.vector.tensor_copy if (half == 0 and t % 2 == 1) else nc.scalar.copy
+                copy_out(y[:, t, :], y_banks[half, t][:])
+                if t % 2 == 1:
+                    nc.sync.dma_start(y_rows[:, t - 1 : t + 1, cols], y[:, t - 1 : t + 1, :])
+            woven = ring.tile([P, HALF, 4], BF16, name="y_woven", tag="wide_bf16", align_bytes=64)
+            interleave(nc.vector.tensor_copy, woven[:], y[:])
+            nc.vector.quantize_mx(
+                out=y_w[:, cols].bitcast(E4), scales=y_s[:, cols], in_=woven[:].rearrange("p m t -> p (m t)")
+            )
+            nc.sync.dma_start(
+                out_1[0].rearrange("p m t -> p (m t)").bitcast(I32)[:, cols], y_w[:, cols].bitcast(I32)
+            )
+        for q in range(4):
+            queue = nc.sync if q % 2 == 0 else nc.scalar
+            queue.dma_start(out_2[0, 4 * q : 4 * q + 4, :].bitcast(I32), y_s[32 * q : 32 * q + 4, :].bitcast(I32))

@@ -11,18 +11,27 @@ I32 = mybir.dt.int32
 U32 = mybir.dt.uint32
 U16 = mybir.dt.uint16
 U8 = mybir.dt.uint8
-E4 = mybir.dt.float8_e4m3fn_x4
-E2 = mybir.dt.float4_e2m1fn_x4
+E4M3 = mybir.dt.float8_e4m3fn_x4
+E2M1 = mybir.dt.float4_e2m1fn_x4
 MULT = mybir.AluOpType.mult
 ADD = mybir.AluOpType.add
-COPY = mybir.ActivationFunctionType.Copy
 
 P = 128
-KA = K // 512
-HB = H // 512
+PASS = 512
+K_PASSES = K // PASS
+R_GROUPS = H // PASS
 SLICES = H // P
-HALF = 512
-B_LEAD = 3
+QUADRANTS = 4
+BANK = 512
+QUARTER = T2 // 4
+H_BANKS = 4
+
+B_FIRST = 6
+B_AHEAD = 2
+PRODUCT_AHEAD = 4
+H_BUFS = 4
+VOL_BUFS = 8
+ROUND_W1_AT = (0, 3, 7)
 
 
 def tile_list_luggage_slot_features_kernel(
@@ -36,288 +45,258 @@ def tile_list_luggage_slot_features_kernel(
         ring = ctx.enter_context(tc.tile_pool(name="ring", bufs=2))
         psum = ctx.enter_context(tc.psum_pool(name="psum", bufs=1))
 
-        idx = lists.tile([P, S // 16], U16, name="idx")
-        idx_a = lists.tile([P, S // 16], U16, name="idx_a")
-        idx_b = lists.tile([P, S // 16], U16, name="idx_b")
+        halves = [slice(BANK * i, BANK * (i + 1)) for i in range(2)]
+        quarters = [slice(QUARTER * i, QUARTER * (i + 1)) for i in range(4)]
 
-        tab_s = held.tile([P, KA, T], U8, name="tab_s", align_bytes=64)
-        w2_s_raw = held.tile([P, KA, H], U8, name="w2_s_raw", align_bytes=64)
+        idx_table = lists.tile([P, S // 16], U16, name="idx_table")
+        idx_page = {side: lists.tile([P, S // 16], U16, name=f"idx_page_{side}") for side in "AB"}
+
+        tab_s = held.tile([P, K_PASSES, T], U8, name="tab_s", align_bytes=64)
+        w2_s_raw = held.tile([P, K_PASSES, H], U8, name="w2_s_raw", align_bytes=64)
         w3_s_raw = held.tile([P, N], U8, name="w3_s_raw", align_bytes=64)
         nc.vector.memset(tab_s[:].bitcast(I32), 0)
         nc.gpsimd.memset(w2_s_raw[:].bitcast(I32), 0)
-        nc.gpsimd.memset(w3_s_raw[:].bitcast(I32), 0)
+        nc.vector.memset(w3_s_raw[:].bitcast(I32), 0)
+
         pages = {}
         for side in "BA":
             pages[side] = [held.tile([P, T2], F32, name=f"page_{side}{i}") for i in range(2)]
             for page in pages[side]:
                 nc.vector.memset(page[:], 0.0)
 
-        nc.sync.dma_start(idx[:], offs)
-        w2_raw = held.tile([P, KA, H // 2], I32, name="w2_raw", tag="raw_words", align_bytes=64)
-        nc.sync.dma_start(w2_raw[:], w2_words.rearrange("a p c -> p a c").bitcast(I32))
-        tab_w = [held.tile([P, T], I32, name=f"tab_w{a}", align_bytes=64) for a in range(KA)]
-
-        def load_tab_words(a):
-            nc.sync.dma_start(tab_w[a][:], tab_words[a].rearrange("p t i -> p (t i)").bitcast(I32))
-
-        load_tab_words(0)
-        for q in range(4):
-            nc.sync.dma_start(
-                tab_s[32 * q : 32 * q + 4, :, :].bitcast(I32),
-                tab_scales[:, 4 * q : 4 * q + 4, :].rearrange("a r c -> r a c").bitcast(I32),
-            )
-        load_tab_words(1)
-        for q in range(4):
-            nc.sync.dma_start(
-                w2_s_raw[32 * q : 32 * q + 4, :, :].bitcast(I32),
-                w2_scales[:, 4 * q : 4 * q + 4, :].rearrange("a r c -> r a c").bitcast(I32),
-            )
-        nc.sync.dma_start(idx_b[:], offs3)
+        def load_scale_rows(tile, scales):
+            for q in range(QUADRANTS):
+                nc.scalar.dma_start(
+                    tile[32 * q : 32 * q + 4, :, :].bitcast(I32),
+                    scales[:, 4 * q : 4 * q + 4, :].rearrange("a r c -> r a c").bitcast(I32),
+                )
 
         gains = {}
 
-        def load_gains(side, wg):
-            gain = held.tile([P, 4, S], F32, name=f"gain_{side}")
-            for q in range(4):
-                nc.sync.dma_start(gain[32 * q : 32 * q + 32, :, :], wg.rearrange("(p t) j -> p t j", t=4))
-            gains[side] = gain
+        def load_gains(side, wg, queue, tag):
+            gains[side] = held.tile([P, 4, S], F32, name=f"gain_{side}", tag=tag)
+            for q in range(QUADRANTS):
+                queue.dma_start(gains[side][32 * q : 32 * q + 32, :, :], wg.rearrange("(p t) j -> p t j", t=4))
 
-        load_gains("B", wg2)
+        nc.sync.dma_start(idx_table[:], offs)
+        w2_raw = held.tile([P, K_PASSES, H // 2], I32, name="w2_raw", tag="w2_raw_then_gain_A")
+        nc.sync.dma_start(w2_raw[:], w2_words.rearrange("a p c -> p a c").bitcast(I32))
+        tab_w = [held.tile([P, T], I32, name=f"tab_w{a}", align_bytes=64) for a in range(K_PASSES)]
+        for a in range(K_PASSES):
+            nc.sync.dma_start(tab_w[a][:], tab_words[a].rearrange("p t i -> p (t i)").bitcast(I32))
+        nc.sync.dma_start(idx_page["B"][:], offs3)
+        load_gains("B", wg2, nc.sync, "gain_B")
+        load_scale_rows(tab_s, tab_scales)
+        load_scale_rows(w2_s_raw, w2_scales)
 
-        nc.sync.dma_start(idx_a[:], offs2)
-        w2_w, w2_s = {}, {}
+        def deal(dealt, raw):
+            nc.vector.tensor_copy(dealt.rearrange("p a t m -> p a m t"), raw.rearrange("p a (m t) -> p a m t", t=4))
 
-        def deal_w2(b):
-            cols = slice(512 * b, 512 * (b + 1))
-            words = held.tile([P, KA, 4, P], U16, name=f"w2_w{b}", align_bytes=64)
-            nc.vector.tensor_copy(
-                words[:].rearrange("p a t m -> p a m t"),
-                w2_raw[:].bitcast(U16)[:, :, cols].rearrange("p a (m t) -> p a m t", t=4),
-            )
-            scales = held.tile([P, KA, 4, P], U8, name=f"w2_s{b}", align_bytes=64)
-            nc.gpsimd.tensor_copy(
-                scales[:].rearrange("p a t m -> p a m t"),
-                w2_s_raw[:, :, cols].rearrange("p a (m t) -> p a m t", t=4),
-            )
-            w2_w[b], w2_s[b] = words, scales
+        w2_w, w2_s = [], []
+        for b in range(R_GROUPS):
+            cols = slice(PASS * b, PASS * (b + 1))
+            w2_w.append(held.tile([P, K_PASSES, 4, P], U16, name=f"w2_w{b}", align_bytes=64))
+            w2_s.append(held.tile([P, K_PASSES, 4, P], U8, name=f"w2_s{b}", align_bytes=64))
+            deal(w2_w[b][:], w2_raw[:].bitcast(U16)[:, :, cols])
+            deal(w2_s[b][:], w2_s_raw[:, :, cols])
 
-        deal_w2(0)
         v_w, v_s = [], []
-        for a in range(KA):
-            words = held.tile([P, S], I32, name=f"v_w{a}", align_bytes=64)
-            scales = held.tile([P, S], U8, name=f"v_s{a}", align_bytes=64)
-            nc.vector.tensor_copy(scales[:], tab_s[:, a, :].indirect(idx[:]))
-            nc.vector.tensor_copy(words[:].bitcast(U32), tab_w[a][:].bitcast(U32).indirect(idx[:]))
-            v_w.append(words)
-            v_s.append(scales)
+        for a in range(K_PASSES):
+            v_w.append(held.tile([P, S], I32, name=f"v_w{a}", align_bytes=64))
+            v_s.append(held.tile([P, S], U8, name=f"v_s{a}", align_bytes=64))
+            nc.vector.tensor_copy(v_s[a][:], tab_s[:, a, :].indirect(idx_table[:]))
+            nc.vector.tensor_copy(v_w[a][:].bitcast(U32), tab_w[a][:].bitcast(U32).indirect(idx_table[:]))
 
-        w1_w, w1_s = {}, {}
+        def quantise(words, scales, woven):
+            nc.vector.quantize_mx(out=words.bitcast(E4M3), scales=scales, in_=woven)
 
-        def prepare_w1(b):
-            for a in range(KA):
-                raw = ring.tile([P, 4, 512], F32, name="w1_raw", tag="wide_f32")
+        w1_raw, w1_bf, w1_w, w1_s = {}, {}, {}, {}
+
+        def load_w1(b):
+            for a in range(K_PASSES):
+                w1_raw[a, b] = ring.tile([P, 4, PASS], F32, name="w1_raw", tag="staged_f32")
                 nc.sync.dma_start(
-                    raw[:],
-                    w1[512 * a : 512 * (a + 1), 512 * b : 512 * (b + 1)].rearrange("(p i) c -> p i c", i=4),
+                    w1_raw[a, b][:],
+                    w1[PASS * a : PASS * (a + 1), PASS * b : PASS * (b + 1)].rearrange("(p i) c -> p i c", i=4),
                 )
-                rounded = ring.tile([P, 4, P, 4], BF16, name="w1_bf", tag="wide_bf16", align_bytes=64)
-                nc.scalar.copy(
-                    rounded[:].rearrange("p t m i -> p m t i"),
-                    raw[:].rearrange("p i (m t) -> p m t i", t=4),
-                )
-                words = held.tile([P, 512], U32, name=f"w1_w{a}{b}", align_bytes=64)
-                scales = held.tile([P, 512], U8, name=f"w1_s{a}{b}", align_bytes=64)
-                nc.vector.quantize_mx(
-                    out=words[:].bitcast(E4), scales=scales[:], in_=rounded[:].rearrange("p t m i -> p (t m i)")
-                )
-                w1_w[a, b], w1_s[a, b] = words, scales
 
-        w3 = {}
+        def round_w1(b, a):
+            if a == 0:
+                w1_bf[b] = held.tile([P, K_PASSES, 4, P, 4], BF16, name="w1_bf", tag="staged_bf16", align_bytes=64)
+            nc.scalar.copy(
+                w1_bf[b][:, a].rearrange("p t m i -> p m t i"),
+                w1_raw[a, b][:].rearrange("p i (m t) -> p m t i", t=4),
+            )
+            if a == K_PASSES - 1:
+                w1_w[b] = held.tile([P, K_PASSES * PASS], U32, name=f"w1_w{b}", align_bytes=64)
+                w1_s[b] = held.tile([P, K_PASSES * PASS], U8, name=f"w1_s{b}", align_bytes=64)
+                quantise(w1_w[b][:], w1_s[b][:], w1_bf[b][:].rearrange("p a t m i -> p (a t m i)"))
+
+        w3_w = held.tile([P, R_GROUPS, 4, P], I32, name="w3_w", align_bytes=64)
+        w3_s = held.tile([P, 1, 4, P], U8, name="w3_s", align_bytes=64)
 
         def prepare_w3():
-            raw = held.tile([P, HB, N], I32, name="w3_raw", tag="raw_words", align_bytes=64)
-            nc.sync.dma_start(raw[:], w3_words.rearrange("a p c i -> p a (c i)").bitcast(I32))
-            for q in range(4):
+            w3_raw = held.tile([P, R_GROUPS, N], I32, name="w3_raw", align_bytes=64)
+            nc.sync.dma_start(w3_raw[:], w3_words.rearrange("a p c i -> p a (c i)").bitcast(I32))
+            for q in range(QUADRANTS):
                 nc.sync.dma_start(
-                    w3_s_raw[32 * q : 32 * q + 4 * HB, :].bitcast(I32),
+                    w3_s_raw[32 * q : 32 * q + 4 * R_GROUPS, :].bitcast(I32),
                     w3_scales[:, 4 * q : 4 * q + 4, :].bitcast(I32),
                 )
-            words = held.tile([P, HB, 4, P], I32, name="w3_w", align_bytes=64)
-            nc.vector.tensor_copy(
-                words[:].rearrange("p a t m -> p a m t"), raw[:].rearrange("p a (m t) -> p a m t", t=4)
-            )
-            scales = held.tile([P, 4, P], U8, name="w3_s", align_bytes=64)
-            nc.vector.tensor_copy(
-                scales[:].rearrange("p t m -> p m t"), w3_s_raw[:].rearrange("p (m t) -> p m t", t=4)
-            )
-            w3["w"], w3["s"] = words, scales
+            deal(w3_w[:], w3_raw[:])
+            deal(w3_s[:], w3_s_raw[:].rearrange("p (a c) -> p a c", a=1))
 
-        steps = [("B", s) for s in range(B_LEAD)]
-        for s in range(SLICES):
-            steps.append(("A", s))
-            if s + B_LEAD < SLICES:
-                steps.append(("B", s + B_LEAD))
-        last = len(steps) - 1
-
-        h_sb, gained, weighted, z4 = {}, {}, {}, {}
         vols = {}
 
         def load_vol(s):
             b, t = divmod(s, 4)
-            rows = ring.tile([P, T2], F32, name="vol_rows", bufs=4)
-            nc.sync.dma_start(rows[:], vol[512 * b : 512 * (b + 1), :].rearrange("(p t) m -> p t m", t=4)[:, t, :])
-            vols[s] = rows
+            vols[s] = ring.tile([P, T2], F32, name="vol_rows", bufs=VOL_BUFS)
+            nc.sync.dma_start(vols[s][:], vol[PASS * b : PASS * (b + 1), :].rearrange("(p t) m -> p t m", t=4)[:, t, :])
+
+        def loads_before_rounding(b):
+            load_w1(b)
+            if b == 0:
+                load_vol(0)
+                load_gains("A", wg1, nc.scalar, "w2_raw_then_gain_A")
+                nc.sync.dma_start(idx_page["A"][:], offs2)
+                for s in range(1, 4):
+                    load_vol(s)
+            elif b == 1:
+                load_vol(4)
+                prepare_w3()
+                load_vol(5)
+            else:
+                for s in range(6, VOL_BUFS):
+                    load_vol(s)
+
+        steps = [("B", s) for s in range(B_FIRST)]
+        for s in range(SLICES):
+            if B_FIRST <= s + B_AHEAD < SLICES:
+                steps.append(("B", s + B_AHEAD))
+            steps.append(("A", s))
+        last = len(steps) - 1
+
+        h_sb = {}
 
         def first_product(k):
             side, s = steps[k]
             b, t = divmod(s, 4)
-            bank = psum.tile([P, S], F32, name="h_bank", tag=f"bank{k % 4}")
-            for a in range(KA):
+            bank = psum.tile([P, S], F32, name="h_bank", tag=f"bank{k % H_BANKS}")
+            for a in range(K_PASSES):
                 if side == "B":
-                    lhs = w2_w[b][:, a, t, :].bitcast(E2)
-                    lhs_s = w2_s[b][:, a, t, :]
+                    weights, weight_scales = w2_w[b][:, a, t, :].bitcast(E2M1), w2_s[b][:, a, t, :]
                 else:
-                    lhs = w1_w[a, b][:, P * t : P * (t + 1)].bitcast(E4)
-                    lhs_s = w1_s[a, b][:, P * t : P * (t + 1)]
+                    cols = slice(PASS * a + P * t, PASS * a + P * (t + 1))
+                    weights, weight_scales = w1_w[b][:, cols].bitcast(E4M3), w1_s[b][:, cols]
                 nc.tensor.matmul_mx(
-                    out=bank[:], lhsT=lhs, lhsT_scale=lhs_s, rhs=v_w[a][:].bitcast(E4), rhs_scale=v_s[a][:],
-                    start=(a == 0), stop=(a == KA - 1),
+                    out=bank[:], lhsT=weights, lhsT_scale=weight_scales,
+                    rhs=v_w[a][:].bitcast(E4M3), rhs_scale=v_s[a][:],
+                    start=(a == 0), stop=(a == K_PASSES - 1),
                 )
-            h = ring.tile([P, S], F32, name="h_sb", bufs=3)
-            nc.scalar.copy(h[:], bank[:])
-            h_sb[k] = h
-
-        def gain_product(k):
-            side, s = steps[k]
-            if k == 0:
-                return
-            g = ring.tile([P, S], F32, name="gained", bufs=3)
-            nc.gpsimd.tensor_tensor(g[:], h_sb[k][:], gains[side][:, s % 4, :], MULT)
-            gained[k] = g
-
-        def page_of(k):
-            side, s = steps[k]
-            return pages[side][s % 2]
+            h_sb[k] = ring.tile([P, S], F32, name="h_sb", bufs=H_BUFS)
+            nc.scalar.copy(h_sb[k][:], bank[:])
 
         def scatter(k):
             side, s = steps[k]
-            where = page_of(k)[:].indirect((idx_a if side == "A" else idx_b)[:])
-            if k == 0:
-                nc.vector.tensor_tensor(where, h_sb[k][:], gains[side][:, s % 4, :], MULT)
-            else:
-                nc.vector.tensor_copy(where, gained[k][:])
+            places = pages[side][s % 2][:].indirect(idx_page[side][:])
+            nc.vector.tensor_tensor(places, h_sb[k][:], gains[side][:, s % 4, :], MULT)
 
-        z_w, z_s = {}, {}
-        y_banks = {}
-
-        def last_pass(b, half):
-            for t in range(4):
-                if b == 0:
-                    y_banks[half, t] = psum.tile(
-                        [P, HALF], F32, name="y_bank", tag=f"bank{4 + t if half == 0 else t}"
-                    )
-                nc.tensor.matmul_mx(
-                    out=y_banks[half, t][:],
-                    lhsT=w3["w"][:, b, t, :].bitcast(E4), lhsT_scale=w3["s"][4 * b : P, t, :],
-                    rhs=z_w[b, half][:].bitcast(E4), rhs_scale=z_s[b, half][:],
-                    start=(b == 0), stop=(b == HB - 1),
-                )
-
-        def interleave(engine_copy, dst, src):
-            engine_copy(dst.rearrange("p (c i) t -> p c t i", i=4), src.rearrange("p t (c i) -> p c t i", i=4))
-
-        def quantise_z(b, half, engine_copy):
-            woven = ring.tile([P, HALF, 4], BF16, name="z_woven", align_bytes=64)
-            interleave(engine_copy, woven[:], z4[b][half][:])
-            words = held.tile([P, HALF], U32, name=f"z_w{b}{half}", align_bytes=64)
-            scales = held.tile([P, HALF], U8, name=f"z_s{b}{half}", align_bytes=64)
-            nc.vector.quantize_mx(
-                out=words[:].bitcast(E4), scales=scales[:], in_=woven[:].rearrange("p m t -> p (m t)")
-            )
-            z_w[b, half], z_s[b, half] = words, scales
+        z_rows = {}
+        z_woven = held.tile([P, T2, 4], BF16, name="z_woven", align_bytes=64)
+        z_w = [held.tile([P, T2], U32, name=f"z_w{b}", align_bytes=64) for b in range(R_GROUPS)]
+        z_s = [held.tile([P, T2], U8, name=f"z_s{b}", align_bytes=64) for b in range(R_GROUPS)]
 
         def combine(k):
             side, s = steps[k]
             b, t = divmod(s, 4)
-            page = page_of(k)
+            page = pages[side][s % 2]
             if side == "B":
-                u = ring.tile([P, T2], F32, name="weighted", bufs=5)
-                nc.scalar.activation(u[:], page[:], COPY, bias=1.0)
-                nc.gpsimd.tensor_tensor(u[:], u[:], vols[s][:], MULT)
-                weighted[s] = u
+                nc.vector.scalar_tensor_tensor(vols[s][:], page[:], 1.0, vols[s][:], ADD, MULT)
                 return
             if t == 0:
-                z4[b] = [ring.tile([P, 4, HALF], BF16, name="z_rows", bufs=4) for half in range(2)]
+                z_rows[b] = ring.tile([P, 4, T2], BF16, name="z_rows")
+            for cols in halves if k == last else [slice(0, T2)]:
+                nc.vector.scalar_tensor_tensor(z_rows[b][:, t, cols], page[:, cols], 1.0, vols[s][:, cols], ADD, MULT)
+
+        def weave(copy, woven, rows):
+            copy(woven.rearrange("p (c i) t -> p c t i", i=4), rows.rearrange("p t (c i) -> p c t i", i=4))
+
+        def flat(woven, cols):
+            return woven[:, cols, :].rearrange("p m t -> p (m t)")
+
+        y_banks = {}
+
+        def last_product(b, half):
+            for t in range(4):
+                if b == 0:
+                    bank = H_BANKS + t if half == 0 else t
+                    y_banks[half, t] = psum.tile([P, BANK], F32, name="y_bank", tag=f"bank{bank}")
+                nc.tensor.matmul_mx(
+                    out=y_banks[half, t][:],
+                    lhsT=w3_w[:, b, t, :].bitcast(E4M3), lhsT_scale=w3_s[4 * b : P, 0, t, :],
+                    rhs=z_w[b][:, halves[half]].bitcast(E4M3), rhs_scale=z_s[b][:, halves[half]],
+                    start=(b == 0), stop=(b == R_GROUPS - 1),
+                )
+
+        def weave_z(b, half):
+            weave(nc.scalar.copy, z_woven[:, halves[half], :], z_rows[b][:, :, halves[half]])
+            if half == 1:
+                quantise(z_w[b][:], z_s[b][:], flat(z_woven, slice(0, T2)))
+                last_product(b, 0)
+
+        weave_at = {}
+        for b in range(R_GROUPS - 1):
+            for half in range(2):
+                weave_at[steps.index(("A", 4 * b + 3)) + 1 + half] = (b, half)
+
+        loads_before_rounding(0)
+        for k in range(-PRODUCT_AHEAD, len(steps)):
             if k == last:
-                for half in range(2):
-                    cols = slice(HALF * half, HALF * (half + 1))
-                    nc.vector.scalar_tensor_tensor(
-                        z4[b][half][:, t, :], page[:, cols], 1.0, weighted[s][:, cols], ADD, MULT
-                    )
-            else:
-                one_plus = ring.tile([P, T2], F32, name="one_plus", bufs=2)
-                nc.scalar.activation(one_plus[:], page[:], COPY, bias=1.0)
-                for half in range(2):
-                    cols = slice(HALF * half, HALF * (half + 1))
-                    nc.gpsimd.tensor_tensor(z4[b][half][:, t, :], one_plus[:, cols], weighted[s][:, cols], MULT)
-            if t == 3 and k != last:
-                for half in range(2):
-                    quantise_z(b, half, nc.scalar.copy)
-                last_pass(b, 0)
+                for b in range(R_GROUPS - 1):
+                    last_product(b, 1)
+            if k >= 0:
+                combine(k)
+                side, s = steps[k]
+                if side == "A" and s + VOL_BUFS < SLICES:
+                    load_vol(s + VOL_BUFS)
+            if k in weave_at:
+                weave_z(*weave_at[k])
+            for b in range(R_GROUPS):
+                for a in range(K_PASSES):
+                    if k == ROUND_W1_AT[b] + a:
+                        round_w1(b, a)
+                        if a == K_PASSES - 1 and b + 1 < R_GROUPS:
+                            loads_before_rounding(b + 1)
+            if k + PRODUCT_AHEAD <= last:
+                first_product(k + PRODUCT_AHEAD)
+            if 0 <= k + 1 <= last:
+                scatter(k + 1)
 
-        deal_w2(1)
-        deal_w2(2)
-        prepare_w1(0)
-        load_gains("A", wg1)
-        for s in range(4):
-            load_vol(s)
-        prepare_w3()
+        b = R_GROUPS - 1
+        for half in range(2):
+            for i in (2 * half, 2 * half + 1):
+                copy = nc.scalar.copy if i in (1, 2) else nc.vector.tensor_copy
+                weave(copy, z_woven[:, quarters[i], :], z_rows[b][:, :, quarters[i]])
+            quantise(z_w[b][:, halves[half]], z_s[b][:, halves[half]], flat(z_woven, halves[half]))
+            last_product(b, half)
 
-        for tick in range(-3, len(steps)):
-            k = tick + 3
-            if k <= last:
-                first_product(k)
-            k = tick + 2
-            if 0 <= k <= last:
-                gain_product(k)
-            k = tick + 1
-            if 0 <= k <= last:
-                scatter(k)
-            if tick >= 0:
-                side, s = steps[tick]
-                if tick == last:
-                    for b in range(HB - 1):
-                        last_pass(b, 1)
-                combine(tick)
-                if side == "B" and s + 4 < SLICES:
-                    load_vol(s + 4)
-                if side == "B" and s in (1, 5):
-                    prepare_w1(s // 4 + 1)
-
-        b = HB - 1
-        quantise_z(b, 0, nc.vector.tensor_copy)
-        quantise_z(b, 1, nc.scalar.copy)
+        y_woven = held.tile([P, T2, 4], BF16, name="y_woven", tag="staged_bf16", align_bytes=64)
         y_w = held.tile([P, T2], U32, name="y_w", align_bytes=64)
         y_s = held.tile([P, T2], U8, name="y_s", align_bytes=64)
-        y_rows = out_0.rearrange("(p t) m -> p t m", t=4)
+        y_rows_out = out_0.rearrange("(p t) m -> p t m", t=4)
+        y_words_out = out_1[0].rearrange("p m t -> p (m t)").bitcast(I32)
         for half in range(2):
-            last_pass(b, half)
-        for half in range(2):
-            cols = slice(HALF * half, HALF * (half + 1))
-            y = ring.tile([P, 4, HALF], F32, name="y", tag="wide_f32")
+            y = ring.tile([P, 4, BANK], F32, name="y", tag="staged_f32")
             for t in range(4):
-                copy_out = nc.vector.tensor_copy if (half == 0 and t % 2 == 1) else nc.scalar.copy
-                copy_out(y[:, t, :], y_banks[half, t][:])
+                copy = nc.vector.tensor_copy if half == 0 and t % 2 == 1 else nc.scalar.copy
+                copy(y[:, t, :], y_banks[half, t][:])
                 if t % 2 == 1:
-                    nc.sync.dma_start(y_rows[:, t - 1 : t + 1, cols], y[:, t - 1 : t + 1, :])
-            woven = ring.tile([P, HALF, 4], BF16, name="y_woven", tag="wide_bf16", align_bytes=64)
-            interleave(nc.vector.tensor_copy, woven[:], y[:])
-            nc.vector.quantize_mx(
-                out=y_w[:, cols].bitcast(E4), scales=y_s[:, cols], in_=woven[:].rearrange("p m t -> p (m t)")
-            )
-            nc.sync.dma_start(
-                out_1[0].rearrange("p m t -> p (m t)").bitcast(I32)[:, cols], y_w[:, cols].bitcast(I32)
-            )
-        for q in range(4):
+                    nc.sync.dma_start(y_rows_out[:, t - 1 : t + 1, halves[half]], y[:, t - 1 : t + 1, :])
+            for i in range(2):
+                cols = quarters[2 * half + i]
+                weave(nc.vector.tensor_copy, y_woven[:, cols, :], y[:, :, quarters[i]])
+                quantise(y_w[:, cols], y_s[:, cols], flat(y_woven, cols))
+                nc.sync.dma_start(y_words_out[:, cols], y_w[:, cols].bitcast(I32))
+        for q in range(QUADRANTS):
             queue = nc.sync if q % 2 == 0 else nc.scalar
             queue.dma_start(out_2[0, 4 * q : 4 * q + 4, :].bitcast(I32), y_s[32 * q : 32 * q + 4, :].bitcast(I32))

@@ -15,6 +15,7 @@ E4M3 = mybir.dt.float8_e4m3fn_x4
 E2M1 = mybir.dt.float4_e2m1fn_x4
 MULT = mybir.AluOpType.mult
 ADD = mybir.AluOpType.add
+COPY = mybir.ActivationFunctionType.Copy
 
 P = 128
 PASS = 512
@@ -28,10 +29,10 @@ H_BANKS = 4
 
 B_FIRST = 6
 B_AHEAD = 2
-PRODUCT_AHEAD = 4
+GAIN_AHEAD = 5
 H_BUFS = 4
 VOL_BUFS = 8
-ROUND_W1_AT = (0, 3, 7)
+ROUND_W1_AT = (-2, 3, 7)
 
 
 def tile_list_luggage_slot_features_kernel(
@@ -54,8 +55,17 @@ def tile_list_luggage_slot_features_kernel(
         tab_s = held.tile([P, K_PASSES, T], U8, name="tab_s", align_bytes=64)
         w2_s_raw = held.tile([P, K_PASSES, H], U8, name="w2_s_raw", align_bytes=64)
         w3_s_raw = held.tile([P, N], U8, name="w3_s_raw", align_bytes=64)
+
+        def load_scale_rows(tile, scales, queue):
+            for q in range(QUADRANTS):
+                queue.dma_start(
+                    tile[32 * q : 32 * q + 4, :, :].bitcast(I32),
+                    scales[:, 4 * q : 4 * q + 4, :].rearrange("a r c -> r a c").bitcast(I32),
+                )
+
         nc.vector.memset(tab_s[:].bitcast(I32), 0)
         nc.gpsimd.memset(w2_s_raw[:].bitcast(I32), 0)
+        load_scale_rows(w2_s_raw, w2_scales, nc.gpsimd)
         nc.vector.memset(w3_s_raw[:].bitcast(I32), 0)
 
         pages = {}
@@ -63,13 +73,6 @@ def tile_list_luggage_slot_features_kernel(
             pages[side] = [held.tile([P, T2], F32, name=f"page_{side}{i}") for i in range(2)]
             for page in pages[side]:
                 nc.vector.memset(page[:], 0.0)
-
-        def load_scale_rows(tile, scales):
-            for q in range(QUADRANTS):
-                nc.scalar.dma_start(
-                    tile[32 * q : 32 * q + 4, :, :].bitcast(I32),
-                    scales[:, 4 * q : 4 * q + 4, :].rearrange("a r c -> r a c").bitcast(I32),
-                )
 
         gains = {}
 
@@ -86,19 +89,24 @@ def tile_list_luggage_slot_features_kernel(
             nc.sync.dma_start(tab_w[a][:], tab_words[a].rearrange("p t i -> p (t i)").bitcast(I32))
         nc.sync.dma_start(idx_page["B"][:], offs3)
         load_gains("B", wg2, nc.sync, "gain_B")
-        load_scale_rows(tab_s, tab_scales)
-        load_scale_rows(w2_s_raw, w2_scales)
+        load_scale_rows(tab_s, tab_scales, nc.scalar)
 
-        def deal(dealt, raw):
-            nc.vector.tensor_copy(dealt.rearrange("p a t m -> p a m t"), raw.rearrange("p a (m t) -> p a m t", t=4))
+        def deal_words(dealt, raw, run):
+            nc.vector.tensor_copy(
+                dealt.rearrange("p a t (c i) -> p a c t i", i=run),
+                raw.rearrange("p a (c i t) -> p a c t i", t=4, i=run),
+            )
+
+        def deal_scales(dealt, raw):
+            nc.gpsimd.tensor_copy(dealt, raw.rearrange("p a (m t) -> p a t m", t=4))
 
         w2_w, w2_s = [], []
         for b in range(R_GROUPS):
             cols = slice(PASS * b, PASS * (b + 1))
             w2_w.append(held.tile([P, K_PASSES, 4, P], U16, name=f"w2_w{b}", align_bytes=64))
             w2_s.append(held.tile([P, K_PASSES, 4, P], U8, name=f"w2_s{b}", align_bytes=64))
-            deal(w2_w[b][:], w2_raw[:].bitcast(U16)[:, :, cols])
-            deal(w2_s[b][:], w2_s_raw[:, :, cols])
+            deal_words(w2_w[b][:], w2_raw[:].bitcast(U16)[:, :, cols], 8)
+            deal_scales(w2_s[b][:], w2_s_raw[:, :, cols])
 
         v_w, v_s = [], []
         for a in range(K_PASSES):
@@ -143,8 +151,8 @@ def tile_list_luggage_slot_features_kernel(
                     w3_s_raw[32 * q : 32 * q + 4 * R_GROUPS, :].bitcast(I32),
                     w3_scales[:, 4 * q : 4 * q + 4, :].bitcast(I32),
                 )
-            deal(w3_w[:], w3_raw[:])
-            deal(w3_s[:], w3_s_raw[:].rearrange("p (a c) -> p a c", a=1))
+            deal_words(w3_w[:], w3_raw[:], 4)
+            deal_scales(w3_s[:], w3_s_raw[:].rearrange("p (a c) -> p a c", a=1))
 
         vols = {}
 
@@ -156,8 +164,8 @@ def tile_list_luggage_slot_features_kernel(
         def loads_before_rounding(b):
             load_w1(b)
             if b == 0:
-                load_vol(0)
                 load_gains("A", wg1, nc.scalar, "w2_raw_then_gain_A")
+                load_vol(0)
                 nc.sync.dma_start(idx_page["A"][:], offs2)
                 for s in range(1, 4):
                     load_vol(s)
@@ -176,7 +184,8 @@ def tile_list_luggage_slot_features_kernel(
             steps.append(("A", s))
         last = len(steps) - 1
 
-        h_sb = {}
+        step_tiles = [held.tile([P, T2], F32, name=f"step_tile{i}") for i in range(GAIN_AHEAD)]
+        h = {}
 
         def first_product(k):
             side, s = steps[k]
@@ -193,13 +202,21 @@ def tile_list_luggage_slot_features_kernel(
                     rhs=v_w[a][:].bitcast(E4M3), rhs_scale=v_s[a][:],
                     start=(a == 0), stop=(a == K_PASSES - 1),
                 )
-            h_sb[k] = ring.tile([P, S], F32, name="h_sb", bufs=H_BUFS)
-            nc.scalar.copy(h_sb[k][:], bank[:])
+            if k == 0:
+                h[k] = bank
+            else:
+                h[k] = ring.tile([P, S], F32, name="h_sb", bufs=H_BUFS)
+                nc.scalar.copy(h[k][:], bank[:])
+
+        def gain_product(k):
+            side, s = steps[k]
+            engine = nc.vector if k == 0 else nc.gpsimd
+            engine.tensor_tensor(step_tiles[k % GAIN_AHEAD][:, :S], h[k][:], gains[side][:, s % 4, :], MULT)
 
         def scatter(k):
             side, s = steps[k]
             places = pages[side][s % 2][:].indirect(idx_page[side][:])
-            nc.vector.tensor_tensor(places, h_sb[k][:], gains[side][:, s % 4, :], MULT)
+            nc.vector.tensor_copy(places, step_tiles[k % GAIN_AHEAD][:, :S])
 
         z_rows = {}
         z_woven = held.tile([P, T2, 4], BF16, name="z_woven", align_bytes=64)
@@ -210,13 +227,18 @@ def tile_list_luggage_slot_features_kernel(
             side, s = steps[k]
             b, t = divmod(s, 4)
             page = pages[side][s % 2]
-            if side == "B":
-                nc.vector.scalar_tensor_tensor(vols[s][:], page[:], 1.0, vols[s][:], ADD, MULT)
-                return
-            if t == 0:
+            if side == "A" and t == 0:
                 z_rows[b] = ring.tile([P, 4, T2], BF16, name="z_rows")
-            for cols in halves if k == last else [slice(0, T2)]:
-                nc.vector.scalar_tensor_tensor(z_rows[b][:, t, cols], page[:, cols], 1.0, vols[s][:, cols], ADD, MULT)
+            if k == last:
+                for cols in halves:
+                    nc.vector.scalar_tensor_tensor(
+                        z_rows[b][:, t, cols], page[:, cols], 1.0, vols[s][:, cols], ADD, MULT
+                    )
+                return
+            one_plus_page = step_tiles[k % GAIN_AHEAD]
+            nc.scalar.activation(one_plus_page[:], page[:], COPY, bias=1.0)
+            result = vols[s][:] if side == "B" else z_rows[b][:, t, :]
+            nc.gpsimd.tensor_tensor(result, one_plus_page[:], vols[s][:], MULT)
 
         def weave(copy, woven, rows):
             copy(woven.rearrange("p (c i) t -> p c t i", i=4), rows.rearrange("p t (c i) -> p c t i", i=4))
@@ -250,7 +272,7 @@ def tile_list_luggage_slot_features_kernel(
                 weave_at[steps.index(("A", 4 * b + 3)) + 1 + half] = (b, half)
 
         loads_before_rounding(0)
-        for k in range(-PRODUCT_AHEAD, len(steps)):
+        for k in range(-GAIN_AHEAD - 1, len(steps)):
             if k == last:
                 for b in range(R_GROUPS - 1):
                     last_product(b, 1)
@@ -267,8 +289,10 @@ def tile_list_luggage_slot_features_kernel(
                         round_w1(b, a)
                         if a == K_PASSES - 1 and b + 1 < R_GROUPS:
                             loads_before_rounding(b + 1)
-            if k + PRODUCT_AHEAD <= last:
-                first_product(k + PRODUCT_AHEAD)
+            if k + GAIN_AHEAD + 1 <= last:
+                first_product(k + GAIN_AHEAD + 1)
+            if 0 <= k + GAIN_AHEAD <= last:
+                gain_product(k + GAIN_AHEAD)
             if 0 <= k + 1 <= last:
                 scatter(k + 1)
 

from contextlib import ExitStack

import concourse.mybir as mybir

K, T, S, T2, H, N = 1024, 2048, 512, 1024, 1536, 512
FLOPS = 2 * (2 * K * H * S + H * N * T2)

F32 = mybir.dt.float32
BF16 = mybir.dt.bfloat16
I32 = mybir.dt.int32
U32 = mybir.dt.uint32
U16 = mybir.dt.uint16
U8 = mybir.dt.uint8
E4M3 = mybir.dt.float8_e4m3fn_x4
E2M1 = mybir.dt.float4_e2m1fn_x4
MULT = mybir.AluOpType.mult
ADD = mybir.AluOpType.add
COPY = mybir.ActivationFunctionType.Copy

P = 128
PASS = 512
K_PASSES = K // PASS
R_GROUPS = H // PASS
SLICES = H // P
QUADRANTS = 4
BANK = 512
QUARTER = T2 // 4
H_BANKS = 4

B_FIRST = 6
B_AHEAD = 2
GAIN_AHEAD = 5
H_BUFS = 4
VOL_BUFS = 8
ROUND_W1_AT = (-2, 3, 7)


def tile_list_luggage_slot_features_kernel(
    tc, tab_words, tab_scales, offs, w1, w2_words, w2_scales, offs2, offs3,
    wg1, wg2, vol, w3_words, w3_scales, out_0, out_1, out_2,
):
    nc = tc.nc
    with ExitStack() as ctx:
        lists = ctx.enter_context(tc.tile_pool(name="lists", bufs=1))
        held = ctx.enter_context(tc.tile_pool(name="held", bufs=1))
        ring = ctx.enter_context(tc.tile_pool(name="ring", bufs=2))
        psum = ctx.enter_context(tc.psum_pool(name="psum", bufs=1))

        halves = [slice(BANK * i, BANK * (i + 1)) for i in range(2)]
        quarters = [slice(QUARTER * i, QUARTER * (i + 1)) for i in range(4)]

        idx_table = lists.tile([P, S // 16], U16, name="idx_table")
        idx_page = {side: lists.tile([P, S // 16], U16, name=f"idx_page_{side}") for side in "AB"}

        tab_s = held.tile([P, K_PASSES, T], U8, name="tab_s", align_bytes=64)
        w2_s_raw = held.tile([P, K_PASSES, H], U8, name="w2_s_raw", align_bytes=64)
        w3_s_raw = held.tile([P, N], U8, name="w3_s_raw", align_bytes=64)

        def load_scale_rows(tile, scales, queue):
            for q in range(QUADRANTS):
                queue.dma_start(
                    tile[32 * q : 32 * q + 4, :, :].bitcast(I32),
                    scales[:, 4 * q : 4 * q + 4, :].rearrange("a r c -> r a c").bitcast(I32),
                )

        nc.vector.memset(tab_s[:].bitcast(I32), 0)
        nc.gpsimd.memset(w2_s_raw[:].bitcast(I32), 0)
        load_scale_rows(w2_s_raw, w2_scales, nc.gpsimd)
        nc.vector.memset(w3_s_raw[:].bitcast(I32), 0)

        pages = {}
        for side in "BA":
            pages[side] = [held.tile([P, T2], F32, name=f"page_{side}{i}") for i in range(2)]
            for page in pages[side]:
                nc.vector.memset(page[:], 0.0)

        gains = {}

        def load_gains(side, wg, queue, tag):
            gains[side] = held.tile([P, 4, S], F32, name=f"gain_{side}", tag=tag)
            for q in range(QUADRANTS):
                queue.dma_start(gains[side][32 * q : 32 * q + 32, :, :], wg.rearrange("(p t) j -> p t j", t=4))

        nc.sync.dma_start(idx_table[:], offs)
        w2_raw = held.tile([P, K_PASSES, H // 2], I32, name="w2_raw", tag="w2_raw_then_gain_A")
        nc.sync.dma_start(w2_raw[:], w2_words.rearrange("a p c -> p a c").bitcast(I32))
        tab_w = [held.tile([P, T], I32, name=f"tab_w{a}", align_bytes=64) for a in range(K_PASSES)]
        for a in range(K_PASSES):
            nc.sync.dma_start(tab_w[a][:], tab_words[a].rearrange("p t i -> p (t i)").bitcast(I32))
        nc.sync.dma_start(idx_page["B"][:], offs3)
        load_gains("B", wg2, nc.sync, "gain_B")
        load_scale_rows(tab_s, tab_scales, nc.scalar)

        def deal_words(dealt, raw, run):
            nc.vector.tensor_copy(
                dealt.rearrange("p a t (c i) -> p a c t i", i=run),
                raw.rearrange("p a (c i t) -> p a c t i", t=4, i=run),
            )

        def deal_scales(dealt, raw):
            nc.gpsimd.tensor_copy(dealt, raw.rearrange("p a (m t) -> p a t m", t=4))

        w2_w, w2_s = [], []
        for b in range(R_GROUPS):
            cols = slice(PASS * b, PASS * (b + 1))
            w2_w.append(held.tile([P, K_PASSES, 4, P], U16, name=f"w2_w{b}", align_bytes=64))
            w2_s.append(held.tile([P, K_PASSES, 4, P], U8, name=f"w2_s{b}", align_bytes=64))
            deal_words(w2_w[b][:], w2_raw[:].bitcast(U16)[:, :, cols], 8)
            deal_scales(w2_s[b][:], w2_s_raw[:, :, cols])

        v_w, v_s = [], []
        for a in range(K_PASSES):
            v_w.append(held.tile([P, S], I32, name=f"v_w{a}", align_bytes=64))
            v_s.append(held.tile([P, S], U8, name=f"v_s{a}", align_bytes=64))
            nc.vector.tensor_copy(v_s[a][:], tab_s[:, a, :].indirect(idx_table[:]))
            nc.vector.tensor_copy(v_w[a][:].bitcast(U32), tab_w[a][:].bitcast(U32).indirect(idx_table[:]))

        def quantise(words, scales, woven):
            nc.vector.quantize_mx(out=words.bitcast(E4M3), scales=scales, in_=woven)

        w1_raw, w1_bf, w1_w, w1_s = {}, {}, {}, {}

        def load_w1(b):
            for a in range(K_PASSES):
                w1_raw[a, b] = ring.tile([P, 4, PASS], F32, name="w1_raw", tag="staged_f32")
                nc.sync.dma_start(
                    w1_raw[a, b][:],
                    w1[PASS * a : PASS * (a + 1), PASS * b : PASS * (b + 1)].rearrange("(p i) c -> p i c", i=4),
                )

        def round_w1(b, a):
            if a == 0:
                w1_bf[b] = held.tile([P, K_PASSES, 4, P, 4], BF16, name="w1_bf", tag="staged_bf16", align_bytes=64)
            nc.scalar.copy(
                w1_bf[b][:, a].rearrange("p t m i -> p m t i"),
                w1_raw[a, b][:].rearrange("p i (m t) -> p m t i", t=4),
            )
            if a == K_PASSES - 1:
                w1_w[b] = held.tile([P, K_PASSES * PASS], U32, name=f"w1_w{b}", align_bytes=64)
                w1_s[b] = held.tile([P, K_PASSES * PASS], U8, name=f"w1_s{b}", align_bytes=64)
                quantise(w1_w[b][:], w1_s[b][:], w1_bf[b][:].rearrange("p a t m i -> p (a t m i)"))

        w3_w = held.tile([P, R_GROUPS, 4, P], I32, name="w3_w", align_bytes=64)
        w3_s = held.tile([P, 1, 4, P], U8, name="w3_s", align_bytes=64)

        def prepare_w3():
            w3_raw = held.tile([P, R_GROUPS, N], I32, name="w3_raw", align_bytes=64)
            nc.sync.dma_start(w3_raw[:], w3_words.rearrange("a p c i -> p a (c i)").bitcast(I32))
            for q in range(QUADRANTS):
                nc.sync.dma_start(
                    w3_s_raw[32 * q : 32 * q + 4 * R_GROUPS, :].bitcast(I32),
                    w3_scales[:, 4 * q : 4 * q + 4, :].bitcast(I32),
                )
            deal_words(w3_w[:], w3_raw[:], 4)
            deal_scales(w3_s[:], w3_s_raw[:].rearrange("p (a c) -> p a c", a=1))

        vols = {}

        def load_vol(s):
            b, t = divmod(s, 4)
            vols[s] = ring.tile([P, T2], F32, name="vol_rows", bufs=VOL_BUFS)
            nc.sync.dma_start(vols[s][:], vol[PASS * b : PASS * (b + 1), :].rearrange("(p t) m -> p t m", t=4)[:, t, :])

        def loads_before_rounding(b):
            load_w1(b)
            if b == 0:
                load_gains("A", wg1, nc.scalar, "w2_raw_then_gain_A")
                load_vol(0)
                nc.sync.dma_start(idx_page["A"][:], offs2)
                for s in range(1, 4):
                    load_vol(s)
            elif b == 1:
                load_vol(4)
                prepare_w3()
                load_vol(5)
            else:
                for s in range(6, VOL_BUFS):
                    load_vol(s)

        steps = [("B", s) for s in range(B_FIRST)]
        for s in range(SLICES):
            if B_FIRST <= s + B_AHEAD < SLICES:
                steps.append(("B", s + B_AHEAD))
            steps.append(("A", s))
        last = len(steps) - 1

        step_tiles = [held.tile([P, T2], F32, name=f"step_tile{i}") for i in range(GAIN_AHEAD)]
        h = {}

        def first_product(k):
            side, s = steps[k]
            b, t = divmod(s, 4)
            bank = psum.tile([P, S], F32, name="h_bank", tag=f"bank{k % H_BANKS}")
            for a in range(K_PASSES):
                if side == "B":
                    weights, weight_scales = w2_w[b][:, a, t, :].bitcast(E2M1), w2_s[b][:, a, t, :]
                else:
                    cols = slice(PASS * a + P * t, PASS * a + P * (t + 1))
                    weights, weight_scales = w1_w[b][:, cols].bitcast(E4M3), w1_s[b][:, cols]
                nc.tensor.matmul_mx(
                    out=bank[:], lhsT=weights, lhsT_scale=weight_scales,
                    rhs=v_w[a][:].bitcast(E4M3), rhs_scale=v_s[a][:],
                    start=(a == 0), stop=(a == K_PASSES - 1),
                )
            if k == 0:
                h[k] = bank
            else:
                h[k] = ring.tile([P, S], F32, name="h_sb", bufs=H_BUFS)
                nc.scalar.copy(h[k][:], bank[:])

        def gain_product(k):
            side, s = steps[k]
            engine = nc.vector if k == 0 else nc.gpsimd
            engine.tensor_tensor(step_tiles[k % GAIN_AHEAD][:, :S], h[k][:], gains[side][:, s % 4, :], MULT)

        def scatter(k):
            side, s = steps[k]
            places = pages[side][s % 2][:].indirect(idx_page[side][:])
            nc.vector.tensor_copy(places, step_tiles[k % GAIN_AHEAD][:, :S])

        z_rows = {}
        z_woven = held.tile([P, T2, 4], BF16, name="z_woven", align_bytes=64)
        z_w = [held.tile([P, T2], U32, name=f"z_w{b}", align_bytes=64) for b in range(R_GROUPS)]
        z_s = [held.tile([P, T2], U8, name=f"z_s{b}", align_bytes=64) for b in range(R_GROUPS)]

        def combine(k):
            side, s = steps[k]
            b, t = divmod(s, 4)
            page = pages[side][s % 2]
            if side == "A" and t == 0:
                z_rows[b] = ring.tile([P, 4, T2], BF16, name="z_rows")
            if k == last:
                for cols in halves:
                    nc.vector.scalar_tensor_tensor(
                        z_rows[b][:, t, cols], page[:, cols], 1.0, vols[s][:, cols], ADD, MULT
                    )
                return
            one_plus_page = step_tiles[k % GAIN_AHEAD]
            nc.scalar.activation(one_plus_page[:], page[:], COPY, bias=1.0)
            result = vols[s][:] if side == "B" else z_rows[b][:, t, :]
            nc.gpsimd.tensor_tensor(result, one_plus_page[:], vols[s][:], MULT)

        def weave(copy, woven, rows):
            copy(woven.rearrange("p (c i) t -> p c t i", i=4), rows.rearrange("p t (c i) -> p c t i", i=4))

        def flat(woven, cols):
            return woven[:, cols, :].rearrange("p m t -> p (m t)")

        y_banks = {}

        def last_product(b, half):
            for t in range(4):
                if b == 0:
                    bank = H_BANKS + t if half == 0 else t
                    y_banks[half, t] = psum.tile([P, BANK], F32, name="y_bank", tag=f"bank{bank}")
                nc.tensor.matmul_mx(
                    out=y_banks[half, t][:],
                    lhsT=w3_w[:, b, t, :].bitcast(E4M3), lhsT_scale=w3_s[4 * b : P, 0, t, :],
                    rhs=z_w[b][:, halves[half]].bitcast(E4M3), rhs_scale=z_s[b][:, halves[half]],
                    start=(b == 0), stop=(b == R_GROUPS - 1),
                )

        def weave_z(b, half):
            weave(nc.scalar.copy, z_woven[:, halves[half], :], z_rows[b][:, :, halves[half]])
            if half == 1:
                quantise(z_w[b][:], z_s[b][:], flat(z_woven, slice(0, T2)))
                last_product(b, 0)

        weave_at = {}
        for b in range(R_GROUPS - 1):
            for half in range(2):
                weave_at[steps.index(("A", 4 * b + 3)) + 1 + half] = (b, half)

        loads_before_rounding(0)
        for k in range(-GAIN_AHEAD - 1, len(steps)):
            if k == last:
                for b in range(R_GROUPS - 1):
                    last_product(b, 1)
            if k >= 0:
                combine(k)
                side, s = steps[k]
                if side == "A" and s + VOL_BUFS < SLICES:
                    load_vol(s + VOL_BUFS)
            if k in weave_at:
                weave_z(*weave_at[k])
            for b in range(R_GROUPS):
                for a in range(K_PASSES):
                    if k == ROUND_W1_AT[b] + a:
                        round_w1(b, a)
                        if a == K_PASSES - 1 and b + 1 < R_GROUPS:
                            loads_before_rounding(b + 1)
            if k + GAIN_AHEAD + 1 <= last:
                first_product(k + GAIN_AHEAD + 1)
            if 0 <= k + GAIN_AHEAD <= last:
                gain_product(k + GAIN_AHEAD)
            if 0 <= k + 1 <= last:
                scatter(k + 1)

        b = R_GROUPS - 1
        for half in range(2):
            for i in (2 * half, 2 * half + 1):
                copy = nc.scalar.copy if i in (1, 2) else nc.vector.tensor_copy
                weave(copy, z_woven[:, quarters[i], :], z_rows[b][:, :, quarters[i]])
            quantise(z_w[b][:, halves[half]], z_s[b][:, halves[half]], flat(z_woven, halves[half]))
            last_product(b, half)

        y_woven = held.tile([P, T2, 4], BF16, name="y_woven", tag="staged_bf16", align_bytes=64)
        y_w = held.tile([P, T2], U32, name="y_w", align_bytes=64)
        y_s = held.tile([P, T2], U8, name="y_s", align_bytes=64)
        y_rows_out = out_0.rearrange("(p t) m -> p t m", t=4)
        y_words_out = out_1[0].rearrange("p m t -> p (m t)").bitcast(I32)
        for half in range(2):
            y = ring.tile([P, 4, BANK], F32, name="y", tag="staged_f32")
            for t in range(4):
                copy = nc.vector.tensor_copy if half == 0 and t % 2 == 1 else nc.scalar.copy
                copy(y[:, t, :], y_banks[half, t][:])
                if t % 2 == 1:
                    nc.sync.dma_start(y_rows_out[:, t - 1 : t + 1, halves[half]], y[:, t - 1 : t + 1, :])
            for i in range(2):
                cols = quarters[2 * half + i]
                weave(nc.vector.tensor_copy, y_woven[:, cols, :], y[:, :, quarters[i]])
                quantise(y_w[:, cols], y_s[:, cols], flat(y_woven, cols))
                nc.sync.dma_start(y_words_out[:, cols], y_w[:, cols].bitcast(I32))
        for q in range(QUADRANTS):
            queue = nc.sync if q % 2 == 0 else nc.scalar
            queue.dma_start(out_2[0, 4 * q : 4 * q + 4, :].bitcast(I32), y_s[32 * q : 32 * q + 4, :].bitcast(I32))
